import numpy as np
CORES = [122,123,126,250,251,254,378,379,382,506,507,510]
N = 12
TK = 512
D = 128 * N
EPS = 0.01
def setup_inputs(rng):
    return {"x": (rng.standard_normal((N, 128, TK), dtype=np.float32) * (0.5 + np.abs(rng.standard_normal((1, 1, TK), dtype=np.float32))) + rng.standard_normal((1, 1, TK), dtype=np.float32)), "w": (rng.standard_normal((N, 128, 128), dtype=np.float32) / 11)}
def reference(x, w):
    X = x.astype(np.float64)
    mu = X.sum(axis=(0, 1)) / D
    Z = X - mu
    Z = Z / np.sqrt((Z ** 2).sum(axis=(0, 1)) / D + EPS)
    s = sum(w[r].astype(np.float64).T @ Z[r] for r in range(N)).astype(np.float32)
    return {"y": np.broadcast_to(s, (N,) + s.shape)}

from concourse.bass import DstId, RemoteDMATransfer
from concourse.mybir import AluOpType, ActivationFunctionType

TK = 512
BL = 128
NB = TK // BL
D = 128 * 12
EPS = 0.01
W = BL + 3
CH = BL + 4
NLOC = 48

SCRATCH = {
    "xs": ("sbuf", [128, TK], "float32"),
    "xq": ("sbuf", [128, TK], "float32"),
    "wa": ("sbuf", [128, CH], "float32"),
    "send": ("sbuf", [128, NB * CH], "float32"),
    "land1": ("sbuf", [128, 3 * CH], "float32"),
    "landA": ("sbuf", [128, CH], "float32"),
    "landB": ("sbuf", [128, CH], "float32"),
    "hsum": ("sbuf", [128, CH], "float32"),
    "psum2": ("sbuf", [128, CH], "float32"),
    "stt": ("sbuf", [128, 4], "float32"),
    "av": ("sbuf", [128, 4], "float32"),
    "ident": ("sbuf", [128, BL], "float32"),
    "negones": ("sbuf", [128, BL], "float32"),
    "dc": ("sbuf", [128, BL], "float32"),
    "drs": ("sbuf", [128, BL], "float32"),
    "tot": ("sbuf", [128, BL], "float32"),
    "tmp": ("sbuf", [128, BL], "float32"),
    "ysend": ("sbuf", [128, BL], "float32"),
    "land4": ("sbuf", [128, TK], "float32"),
    "ps0": ("psum", [128, 512], "float32"),
    "ps1": ("psum", [128, 512], "float32"),
    "ps2": ("psum", [128, 512], "float32"),
    "ps3": ("psum", [128, 512], "float32"),
    "psc": ("psum", [128, 512], "float32"),
    "pcb": ("psum", [128, 512], "float32"),
    "py": ("psum", [128, 512], "float32"),
}
SEMAPHORES = (["s1_0", "s1_1", "s1_2", "sA", "sB", "s4_0", "s4_1", "s4_2", "s4_3", "loc", "st"]
              + ["q%d" % i for i in range(NLOC)])


def _bits(mask):
    return [b for b in range(16) if (mask >> b) & 1]


def _mask_of(bits):
    m = 0
    for b in bits:
        m |= 1 << b
    return m


def _plan(T, topo):
    group = list(T.cores)
    hosts = sorted(set(topo.host(c) for c in group))
    owners = {}
    for h in hosts:
        rk = sorted(c for c in group if topo.host(c) == h)
        base = h * topo.CORES_PER_HOST
        idle = [c for c in range(base, base + topo.CORES_PER_HOST)
                if topo.chip(c) == topo.chip(rk[0]) and c not in group]
        helper = min(idle, key=lambda c: (sum(1 for r in rk if topo.die(r) == topo.die(c)), c))
        owners[h] = [helper] + rk
    first, second = {}, {}
    for h in hosts:
        me = owners[h][0]
        sw = [k for k in hosts if k != h and topo.rack(k) == topo.rack(h)][0]
        cb = [k for k in hosts if topo.rack(k) != topo.rack(h) and topo.may_write(me, owners[k][0])][0]
        first[h], second[h] = {}, {}
        seen = {}
        for c in sorted(owners[h]):
            k = seen.get(topo.die(c), 0)
            seen[topo.die(c)] = k + 1
            q = owners[h].index(c)
            first[h][q], second[h][q] = (sw, cb) if k % 2 == 0 else (cb, sw)
    return owners, first, second


def rank_program(g, core, T, topo):
    owners, first, second = _plan(T, topo)
    h = topo.host(core)
    if h not in owners or core not in owners[h]:
        return
    own = owners[h].index(core)
    is_rank = T.rank_of(core) is not None
    ranks = owners[h][1:]
    V, S, P, Y = g.vector, g.scalar, g.tensor, g.sync
    mult, add, sub = AluOpType.mult, AluOpType.add, AluOpType.subtract
    n = [0]

    def new():
        n[0] += 1
        return T.sem["q%d" % (n[0] - 1)]

    def chunk(buf, k, lo=0, hi=W):
        return buf[:, k * CH + lo:k * CH + hi]

    loc_total = 0
    ps = [T.ps0, T.ps1, T.ps2, T.ps3]

    e_one, e_id, e_neg = new(), new(), new()
    if is_rank:
        e_k, e_x, e_w = new(), new(), new()
        Y.dma_start(T.xs[:], T.x[:]).then_inc(e_x, 16)
        S.dma_start(T.wa[:, 0:BL], T.w[:]).then_inc(e_w, 16)
        V.memset(T.wa[:, BL:BL + 1], 1.0 / D).then_inc(e_k, 1)
        V.memset(T.wa[:, BL + 1:BL + 2], 1.0).then_inc(e_k, 1)
    V.memset(T.ident[:], 1.0).then_inc(e_one, 1)
    V.memset(T.negones[:], -1.0).then_inc(e_neg, 1)
    g.wait_ge(e_one, 1)
    g.affine_select(T.ident[:], T.ident[:], [[-1, BL]], AluOpType.is_equal, 0.0, 0, 1).then_inc(e_id, 1)

    if is_rank:
        i = own - 1
        order = [0, (i + 1) % 3 + 1, (i + 2) % 3 + 1, own]
        e_c = new()
        e_mm = {q: new() for q in order}
        e_sq = {q: new() for q in order}
        e_cp = {q: new() for q in order}
        P.wait_ge(e_w, 16)
        P.wait_ge(e_k, 2)
        P.matmul(T.psc[:, 0:1], T.wa[:, 0:BL], T.wa[:, BL + 1:BL + 2], True, True).then_inc(e_c, 1)
        V.wait_ge(e_c, 1)
        for q in order:
            V.tensor_copy(chunk(T.send, q, BL + 2, BL + 3), T.psc[:, 0:1]).then_inc(e_cp[q], 1)
        S.wait_ge(e_x, 16)
        P.wait_ge(e_x, 16)
        for q in order:
            blk = slice(q * BL, (q + 1) * BL)
            S.activation(T.xq[:, blk], T.xs[:, blk], ActivationFunctionType.Square).then_inc(e_sq[q], 1)
            P.matmul(ps[q][:, 0:BL + 1], T.xs[:, blk], T.wa[:, 0:BL + 1], True, True).then_inc(e_mm[q], 1)
            P.wait_ge(e_sq[q], 1)
            P.matmul(ps[q][:, BL + 1:BL + 2], T.xq[:, blk], T.wa[:, BL:BL + 1], True, True).then_inc(e_mm[q], 1)
            V.wait_ge(e_mm[q], 2)
            V.tensor_copy(chunk(T.send, q, 0, BL + 2), ps[q][:, 0:BL + 2]).then_inc(e_cp[q], 1)
        for slot, q in enumerate(order[:3]):
            dst = owners[h][q]
            eng = _bits(topo.mask(core, dst))
            half = len(eng) // 2
            use = eng[half:] if slot % 2 else eng[:half]
            rid, pid = topo.addr(dst, core)
            g.wait_ge(e_cp[q], 2)
            g.remote_dma(chunk(T.land1, i), chunk(T.send, q), T.sem["s1_%d" % i], T.sem.loc, pid, rid, _mask_of(use))
            loc_total += len(use)

    e_l1, e_l = new(), new()
    n1 = len(_bits(topo.mask(ranks[0], ranks[1]))) // 2
    if is_rank:
        i = own - 1
        a, b = (i - 1) % 3, (i + 1) % 3
        V.wait_ge(e_cp[own], 2)
        in0 = chunk(T.send, own)
    else:
        a, b = 1, 2
        V.wait_ge(T.sem.s1_0, n1)
        in0 = chunk(T.land1, 0)
    V.wait_ge(T.sem["s1_%d" % a], n1)
    V.tensor_tensor(T.hsum[:, 0:W], in0, chunk(T.land1, a), add).then_inc(e_l1, 1)
    V.wait_ge(e_l1, 1)
    V.wait_ge(T.sem["s1_%d" % b], n1)
    V.tensor_tensor(T.hsum[:, 0:W], T.hsum[:, 0:W], chunk(T.land1, b), add).then_inc(e_l, 1)

    pa = owners[first[h][own]][own]
    pb = owners[second[h][own]][own]
    ma, mb = topo.mask(core, pa), topo.mask(core, pb)
    e_s2 = new()
    rid, pid = topo.addr(pa, core)
    g.wait_ge(e_l, 1)
    g.remote_dma(T.landA[:, 0:W], T.hsum[:, 0:W], T.sem.sA, T.sem.loc, pid, rid, ma)
    loc_total += len(_bits(ma))
    V.wait_ge(e_l, 1)
    V.wait_ge(T.sem.sA, len(_bits(topo.mask(pa, core))))
    V.tensor_tensor(T.psum2[:, 0:W], T.hsum[:, 0:W], T.landA[:, 0:W], add).then_inc(e_s2, 1)
    rid, pid = topo.addr(pb, core)
    g.wait_ge(e_s2, 1)
    g.remote_dma(T.landB[:, 0:W], T.psum2[:, 0:W], T.sem.sB, T.sem.loc, pid, rid, mb)
    loc_total += len(_bits(mb))

    e_st, e_a, e_sd, e_dc, e_cn, e_tot, e_tmp, e_tc, e_rs, e_drs, e_y, e_ys = [new() for _ in range(12)]
    mu, e2, cc = T.stt[:, 0:1], T.stt[:, 1:2], T.stt[:, 2:3]
    V.wait_ge(e_s2, 1)
    V.wait_ge(T.sem.sB, len(_bits(topo.mask(pb, core))))
    V.tensor_tensor(T.stt[:, 0:3], T.psum2[:, BL:W], T.landB[:, BL:W], add).then_inc(e_st, 1)
    V.wait_ge(e_st, 1)
    V.tensor_scalar(T.av[:, 0:1], mu, mu, EPS, mult, sub).then_inc(e_a, 1)
    S.wait_ge(e_st, 1)
    S.wait_ge(e_a, 1)
    S.activation(T.av[:, 1:2], T.av[:, 0:1], ActivationFunctionType.Sqrt, bias=e2, scale=-1.0).then_inc(e_sd, 1)
    V.wait_ge(e_id, 1)
    V.tensor_scalar(T.dc[:], T.ident[:], cc, None, mult).then_inc(e_dc, 1)
    P.wait_ge(e_neg, 1)
    P.wait_ge(e_dc, 1)
    P.matmul(T.pcb[:, 0:BL], T.negones[:], T.dc[:], True, True).then_inc(e_cn, 1)
    V.tensor_tensor(T.tot[:], T.psum2[:, 0:BL], T.landB[:, 0:BL], add).then_inc(e_tot, 1)
    V.wait_ge(e_cn, 1)
    V.tensor_scalar(T.tmp[:], T.pcb[:, 0:BL], mu, None, mult).then_inc(e_tmp, 1)
    V.wait_ge(e_tot, 1)
    V.wait_ge(e_tmp, 1)
    V.tensor_tensor(T.tot[:], T.tot[:], T.tmp[:], add).then_inc(e_tc, 1)
    V.wait_ge(e_sd, 1)
    V.reciprocal(T.av[:, 2:3], T.av[:, 1:2]).then_inc(e_rs, 1)
    V.wait_ge(e_rs, 1)
    V.tensor_scalar(T.drs[:], T.ident[:], T.av[:, 2:3], None, mult).then_inc(e_drs, 1)
    P.wait_ge(e_tc, 1)
    P.wait_ge(e_drs, 1)
    P.matmul(T.py[:, 0:BL], T.tot[:], T.drs[:], True, True).then_inc(e_y, 1)
    V.wait_ge(e_y, 1)
    V.tensor_copy(T.ysend[:], T.py[:, 0:BL]).then_inc(e_ys, 1)

    dsts = [r for r in ranks if r != core]
    m4 = topo.mask(core, dsts[0])
    for r in dsts:
        m4 &= topo.mask(core, r)
    ids = []
    for r in dsts:
        rid, pid = topo.addr(r, core)
        ids.append(DstId(rid=rid, pnc=pid))
    g.wait_ge(e_ys, 1)
    g.remote_dma_fused([RemoteDMATransfer(dst_ids=ids, dma_engine_mask=m4, remote_sem=T.sem["s4_%d" % own],
                                          srcs=[T.ysend[:]],
                                          dsts=[T.land4[:, own * BL:(own + 1) * BL] for _ in dsts])],
                       local_sem=T.sem.loc)
    loc_total += len(_bits(m4))

    if is_rank:
        i = own - 1
        qa, qb = (i + 1) % 3 + 1, (i + 2) % 3 + 1
        Y.wait_ge(e_ys, 1)
        Y.dma_start(T.y[:, own * BL:(own + 1) * BL], T.ysend[:]).then_inc(T.sem.st, 16)
        for queue, q in ((Y, qa), (S, qb), (S, 0)):
            queue.wait_ge(T.sem["s4_%d" % q], len(_bits(topo.mask(owners[h][q], core))))
            queue.dma_start(T.y[:, q * BL:(q + 1) * BL], T.land4[:, q * BL:(q + 1) * BL]).then_inc(T.sem.st, 16)
        g.wait_ge(T.sem.st, 16 * NB)
    g.wait_ge(T.sem.loc, loc_total)
